import numpy as np
import ml_dtypes


def mxq(x, axis, fmt="e4m3"):
    dtype, down = {"e4m3": (ml_dtypes.float8_e4m3fn, 7), "e5m2": (ml_dtypes.float8_e5m2, 14)}[fmt]
    v = np.moveaxis(np.asarray(x, np.float32).astype(ml_dtypes.bfloat16).astype(np.float64), axis, -1)
    blocks = v.reshape(v.shape[:-1] + (-1, 32))
    amax = np.abs(blocks).max(-1, keepdims=True)
    byte = np.maximum(np.where(amax > 0, np.frexp(amax)[1] - 1 + 127, 0) - down, 1)
    scale = np.exp2(byte - 127.0)
    codes = (blocks / scale).astype(np.float32).astype(dtype).astype(np.float64)
    return np.moveaxis((codes * scale).reshape(v.shape), -1, axis)


WIDE = False


def mx_kscale(k):
    if not WIDE:
        return np.ones(k)
    levels = np.array([10, -10, 5, -5, 0])
    if k % 512:
        return np.exp2(np.random.permutation(np.resize(levels, k // 32))).repeat(32)
    a = np.empty((k // 512, 16))
    for p in range(k // 512):
        a[p, :8] = np.random.permutation(np.resize(levels, 8))
        for g in range(8):
            far = levels[np.abs(levels - a[p, g]) >= 10]
            a[p, g + 8] = far[np.random.randint(len(far))]
    return np.exp2(a.ravel()).repeat(32)


def f64(x):
    return np.asarray(x).astype(np.float64)


E2M1 = np.array([0.0, 0.5, 1.0, 1.5, 2.0, 3.0, 4.0, 6.0, -0.0, -0.5, -1.0, -1.5, -2.0, -3.0, -4.0, -6.0])


def pack_weight(w, fmt):
    k, n = w.shape
    w = f64(np.asarray(w, np.float32).astype(ml_dtypes.bfloat16)).reshape(k // 32, 32, n)
    amax = np.abs(w).max(1)
    if fmt == "e4m3":
        byte = np.frexp(amax)[1] - 1 + 127 - 7
    else:
        mant, ex = np.frexp(amax / 6.0)
        byte = np.where(mant > 0.5, ex, ex - 1) + 127
    byte = np.clip(np.where(amax > 0, byte, 1), 1, 254)
    scaled = (w * np.exp2(127.0 - byte)[:, None, :]).reshape(k, n).astype(np.float32)
    by_word = np.ascontiguousarray(scaled.reshape(k // 512, 128, 4, n).transpose(0, 1, 3, 2))
    if fmt == "e4m3":
        words = by_word.astype(ml_dtypes.float8_e4m3fn).view(np.uint8)
    else:
        c = by_word.astype(ml_dtypes.float4_e2m1fn).view(np.uint8) & 0xF
        words = (c[..., 0::2] | (c[..., 1::2] << 4)).reshape(k // 512, 128, 2 * n)
    return np.ascontiguousarray(words), np.ascontiguousarray(byte.astype(np.uint8).reshape(k // 512, 16, n))


def unpack_weight(words, scales, fmt):
    g, _, n = scales.shape
    words = np.ascontiguousarray(words).reshape(g, 128, n, -1)
    if fmt == "e4m3":
        vals = words.view(ml_dtypes.float8_e4m3fn).astype(np.float64)
    else:
        nib = np.empty((g, 128, n, 4), np.uint8)
        nib[..., 0::2] = words & 0xF
        nib[..., 1::2] = words >> 4
        vals = E2M1[nib]
    vals = vals * np.repeat(np.exp2(scales.astype(np.float64) - 127.0), 8, axis=1)[..., None]
    return vals.transpose(0, 1, 3, 2).reshape(g * 512, n)


def sigmoid(v):
    return 1.0 / (1.0 + np.exp(-v))


K, L, M, T, N = 1024, 1024, 512, 512, 512


def setup_inputs():
    n = np.random.standard_normal
    fk = mx_kscale(K)
    fl = mx_kscale(L)
    fm = mx_kscale(M)
    xap = pack_weight(n((K, T)) / fk[:, None], "e4m3")
    wap = pack_weight(n((K, N)) * 1 / np.sqrt(K) * fk[:, None], "e2m1")
    xqp = pack_weight(n((L, T)) / fl[:, None], "e2m1")
    xgp = pack_weight(n((M, T)) / fm[:, None], "e2m1")
    wgp = pack_weight(n((M, N)) * 1 / np.sqrt(M) * fm[:, None], "e4m3")
    return {
        "xa_words": xap[0],
        "xa_scales": xap[1],
        "wa_words": wap[0],
        "wa_scales": wap[1],
        "xq_words": xqp[0],
        "xq_scales": xqp[1],
        "wq": (n((L, N)) * 1 / np.sqrt(L) * fl[:, None]).astype(np.float32),
        "xg_words": xgp[0],
        "xg_scales": xgp[1],
        "wg_words": wgp[0],
        "wg_scales": wgp[1],
    }


def reference(xa_words, xa_scales, wa_words, wa_scales, xq_words, xq_scales, wq, xg_words, xg_scales, wg_words, wg_scales):
    xau = unpack_weight(xa_words, xa_scales, "e4m3")
    wau = unpack_weight(wa_words, wa_scales, "e2m1")
    xqu = unpack_weight(xq_words, xq_scales, "e2m1")
    xgu = unpack_weight(xg_words, xg_scales, "e2m1")
    wgu = unpack_weight(wg_words, wg_scales, "e4m3")
    wqq = mxq(f64(wq), 0, "e4m3")
    p = wau.T @ xau + wqq.T @ xqu
    g = wgu.T @ xgu
    y = p * sigmoid(g) + 0.1 * g
    return y

@@ -1,0 +1,216 @@
+from contextlib import ExitStack
+
+import concourse.mybir as mybir
+
+K, L, M, T, N = 1024, 1024, 512, 512, 512
+FLOPS = 2 * (K + L + M) * T * N
+
+F32 = mybir.dt.float32
+BF16 = mybir.dt.bfloat16
+I32 = mybir.dt.int32
+U32 = mybir.dt.uint32
+U8 = mybir.dt.uint8
+FP8X4 = mybir.dt.float8_e4m3fn_x4
+FP4X4 = mybir.dt.float4_e2m1fn_x4
+ACT = mybir.ActivationFunctionType
+ALU = mybir.AluOpType
+
+P = 128
+PACK = 4
+K_PASS = P * PACK
+TILES = N // P
+GATE_SHARE = 0.1
+
+
+def tile_mix_gate_over_mixed_sum_kernel(
+    tc, xa_words, xa_scales, wa_words, wa_scales, xq_words, xq_scales, wq, xg_words, xg_scales, wg_words, wg_scales, out
+):
+    nc = tc.nc
+    with ExitStack() as ctx:
+        keep = ctx.enter_context(tc.tile_pool(name="keep", bufs=1))
+        psum = ctx.enter_context(tc.psum_pool(name="psum", bufs=1))
+        ctx.enter_context(tc.manual_schedule())
+
+        scale_sources = [xg_scales, wg_scales, xq_scales, wa_scales, xa_scales]
+        first_plane = [0, 1, 2, 4, 6]
+        planes = keep.tile([P, 8 * T], U8, name="planes", align_bytes=64)
+        staged = keep.tile([P, 8 * T], U8, name="staged", align_bytes=64)
+        nc.vector.memset(planes[:].bitcast(I32), 0)
+
+        def load_e4m3(words, name):
+            passes = words.shape[0]
+            t = keep.tile([P, passes, T], U32, name=name, align_bytes=64)
+            nc.sync.dma_start(out=t[:].bitcast(I32), in_=words.rearrange("z p c r -> p z (c r)").bitcast(I32))
+            return t
+
+        def load_e2m1(words, name):
+            passes = words.shape[0]
+            t = keep.tile([P, passes, 2 * T], U8, name=name, align_bytes=64)
+            nc.sync.dma_start(out=t[:].bitcast(I32), in_=words.rearrange("z p c -> p z c").bitcast(I32))
+            return t
+
+        raw = {}
+
+        def load_wq(j, z):
+            t = keep.tile([P, PACK, P], F32, name="raw%d%d" % (j, z), align_bytes=64)
+            rows = wq[z * K_PASS : (z + 1) * K_PASS, j * P : (j + 1) * P]
+            nc.sync.dma_start(out=t[:], in_=rows.rearrange("(p r) n -> p r n", r=PACK))
+            raw[(j, z)] = t
+
+        load_wq(0, 0)
+        for src, first in zip(scale_sources, first_plane):
+            passes = src.shape[0]
+            dst = staged[4:P:8, first * T : (first + passes) * T].bitcast(I32)
+            nc.sync.dma_start(
+                out=dst.rearrange("q (z c) -> q z c", z=passes), in_=src.bitcast(I32).rearrange("z q c -> q z c")
+            )
+        xg = load_e2m1(xg_words, "xg")
+        xa = load_e4m3(xa_words, "xa")
+        wg = load_e4m3(wg_words, "wg")
+        for r in range(4):
+            nc.sync.dma_start(out=planes[r:P:32, :].bitcast(I32), in_=staged[4 + 8 * r : P : 32, :].bitcast(I32))
+        load_wq(0, 1)
+        xq = load_e2m1(xq_words, "xq")
+        wa = load_e2m1(wa_words, "wa")
+        for j in range(1, TILES):
+            for z in range(2):
+                load_wq(j, z)
+
+        def plane(index, cols):
+            return planes[:, index * T + cols.start : index * T + cols.stop]
+
+        grouped = [keep.tile([P, 2, P * PACK], BF16, name="grouped%d" % j, align_bytes=64) for j in range(TILES)]
+        codes = [keep.tile([P, 2 * P], U32, name="codes%d" % j, align_bytes=64) for j in range(TILES)]
+        made = [keep.tile([P, 2 * P], U8, name="made%d" % j, align_bytes=64) for j in range(TILES)]
+        p_bank = [psum.tile([P, T], F32, name="p%d" % j) for j in range(TILES)]
+        g_bank = [psum.tile([P, T], F32, name="g%d" % j) for j in range(TILES)]
+        gate = [keep.tile([P, T], F32, name="gate%d" % j) for j in range(TILES)]
+        gated = [keep.tile([P, T], F32, name="gated%d" % j) for j in range(TILES)]
+        result = [keep.tile([P, T], F32, name="result%d" % j) for j in range(TILES)]
+        everything = slice(0, T)
+
+        def cast(j, z, on_vector):
+            dst = grouped[j][:, z, :].rearrange("p (c i r) -> p c r i", i=4, r=PACK)
+            src = raw[(j, z)][:].rearrange("p r (c i) -> p c r i", i=4)
+            if on_vector:
+                nc.vector.tensor_copy(out=dst, in_=src)
+            else:
+                nc.scalar.copy(out=dst, in_=src)
+
+        def quantise(j, z0, z1):
+            nc.vector.quantize_mx(
+                out=codes[j][:, z0 * P : z1 * P].bitcast(FP8X4),
+                scales=made[j][:, z0 * P : z1 * P],
+                in_=grouped[j][:, z0:z1, :].rearrange("p z c -> p (z c)"),
+            )
+
+        def g_pass(j):
+            cols = slice(j * P, (j + 1) * P)
+            nc.tensor.matmul_mx(
+                out=g_bank[j][:],
+                lhsT=wg[:, 0, cols].bitcast(FP8X4),
+                lhsT_scale=plane(1, cols),
+                rhs=xg[:, 0, :].bitcast(FP4X4),
+                rhs_scale=plane(0, everything),
+                start=True,
+                stop=True,
+            )
+
+        def sigmoid(j):
+            nc.scalar.activation(out=gate[j][:], in_=g_bank[j][:], func=ACT.Sigmoid)
+
+        def a_pass(j, z, start, stop):
+            cols = slice(j * P, (j + 1) * P)
+            nc.tensor.matmul_mx(
+                out=p_bank[j][:],
+                lhsT=wa[:, z, 2 * cols.start : 2 * cols.stop].bitcast(FP4X4),
+                lhsT_scale=plane(4 + z, cols),
+                rhs=xa[:, z, :].bitcast(FP8X4),
+                rhs_scale=plane(6 + z, everything),
+                start=start,
+                stop=stop,
+            )
+
+        def q_pass(j, z, start, stop):
+            nc.tensor.matmul_mx(
+                out=p_bank[j][:],
+                lhsT=codes[j][:, z * P : (z + 1) * P].bitcast(FP8X4),
+                lhsT_scale=made[j][:, z * P : (z + 1) * P],
+                rhs=xq[:, z, :].bitcast(FP4X4),
+                rhs_scale=plane(2 + z, everything),
+                start=start,
+                stop=stop,
+            )
+
+        def mul(j, cols):
+            nc.vector.tensor_tensor(out=gated[j][:, cols], in0=p_bank[j][:, cols], in1=gate[j][:, cols], op=ALU.mult)
+
+        def add(j, cols):
+            nc.vector.scalar_tensor_tensor(
+                out=result[j][:, cols],
+                in0=g_bank[j][:, cols],
+                scalar=GATE_SHARE,
+                in1=gated[j][:, cols],
+                op0=ALU.mult,
+                op1=ALU.add,
+            )
+
+        def store(j, cols):
+            nc.sync.dma_start(out=out[j * P : (j + 1) * P, cols], in_=result[j][:, cols])
+
+        halves = [slice(0, T // 2), slice(T // 2, T)]
+        cast(0, 0, True)
+        quantise(0, 0, 1)
+        cast(0, 1, True)
+        quantise(0, 1, 2)
+        cast(1, 0, True)
+        quantise(1, 0, 1)
+        cast(1, 1, True)
+        quantise(1, 1, 2)
+        g_pass(0)
+        g_pass(1)
+        q_pass(0, 0, True, False)
+        q_pass(0, 1, False, False)
+        a_pass(0, 0, False, False)
+        a_pass(0, 1, False, True)
+        a_pass(1, 0, True, False)
+        a_pass(1, 1, False, False)
+        q_pass(1, 0, False, False)
+        q_pass(1, 1, False, True)
+        g_pass(2)
+        g_pass(3)
+        a_pass(2, 0, True, False)
+        a_pass(2, 1, False, False)
+        a_pass(3, 0, True, False)
+        a_pass(3, 1, False, False)
+        sigmoid(0)
+        sigmoid(1)
+        cast(2, 0, False)
+        cast(2, 1, False)
+        cast(3, 0, False)
+        cast(3, 1, False)
+        sigmoid(2)
+        sigmoid(3)
+        mul(0, everything)
+        quantise(2, 0, 1)
+        add(0, everything)
+        store(0, everything)
+        quantise(2, 1, 2)
+        mul(1, everything)
+        quantise(3, 0, 1)
+        quantise(3, 1, 2)
+        add(1, everything)
+        store(1, everything)
+        q_pass(2, 0, False, False)
+        q_pass(2, 1, False, True)
+        q_pass(3, 0, False, False)
+        q_pass(3, 1, False, True)
+        mul(2, everything)
+        mul(3, halves[0])
+        add(2, everything)
+        store(2, everything)
+        mul(3, halves[1])
+        add(3, halves[0])
+        store(3, halves[0])
+        add(3, halves[1])
+        store(3, halves[1])

@@ -34,7 +34,6 @@ def tile_mix_gate_over_mixed_sum_kernel(
         scale_sources = [xg_scales, wg_scales, xq_scales, wa_scales, xa_scales]
         first_plane = [0, 1, 2, 4, 6]
         planes = keep.tile([P, 8 * T], U8, name="planes", align_bytes=64)
-        staged = keep.tile([P, 8 * T], U8, name="staged", align_bytes=64)
         nc.vector.memset(planes[:].bitcast(I32), 0)
 
         def load_e4m3(words, name):
@@ -51,30 +50,31 @@ def tile_mix_gate_over_mixed_sum_kernel(
 
         raw = {}
 
-        def load_wq(j, z):
-            t = keep.tile([P, PACK, P], F32, name="raw%d%d" % (j, z), align_bytes=64)
-            rows = wq[z * K_PASS : (z + 1) * K_PASS, j * P : (j + 1) * P]
+        def load_wq(j0, j1, z):
+            t = keep.tile([P, PACK, (j1 - j0) * P], F32, name="raw%d%d" % (j0, z), align_bytes=64)
+            rows = wq[z * K_PASS : (z + 1) * K_PASS, j0 * P : j1 * P]
             nc.sync.dma_start(out=t[:], in_=rows.rearrange("(p r) n -> p r n", r=PACK))
-            raw[(j, z)] = t
+            for j in range(j0, j1):
+                raw[(j, z)] = t[:, :, (j - j0) * P : (j - j0 + 1) * P]
 
-        load_wq(0, 0)
+        xg = load_e2m1(xg_words, "xg")
+        load_wq(0, 2, 0)
         for src, first in zip(scale_sources, first_plane):
             passes = src.shape[0]
-            dst = staged[4:P:8, first * T : (first + passes) * T].bitcast(I32)
+            dst = planes[0:P:8, first * T : (first + passes) * T].bitcast(I32)
             nc.sync.dma_start(
                 out=dst.rearrange("q (z c) -> q z c", z=passes), in_=src.bitcast(I32).rearrange("z q c -> q z c")
             )
-        xg = load_e2m1(xg_words, "xg")
         xa = load_e4m3(xa_words, "xa")
         wg = load_e4m3(wg_words, "wg")
-        for r in range(4):
-            nc.sync.dma_start(out=planes[r:P:32, :].bitcast(I32), in_=staged[4 + 8 * r : P : 32, :].bitcast(I32))
-        load_wq(0, 1)
+        for r in range(1, 4):
+            nc.sync.dma_start(out=planes[r:P:32, :].bitcast(I32), in_=planes[8 * r : P : 32, :].bitcast(I32))
+        load_wq(0, 2, 1)
         xq = load_e2m1(xq_words, "xq")
         wa = load_e2m1(wa_words, "wa")
-        for j in range(1, TILES):
+        for j in range(2, TILES):
             for z in range(2):
-                load_wq(j, z)
+                load_wq(j, j + 1, z)
 
         def plane(index, cols):
             return planes[:, index * T + cols.start : index * T + cols.stop]
@@ -91,7 +91,7 @@ def tile_mix_gate_over_mixed_sum_kernel(
 
         def cast(j, z, on_vector):
             dst = grouped[j][:, z, :].rearrange("p (c i r) -> p c r i", i=4, r=PACK)
-            src = raw[(j, z)][:].rearrange("p r (c i) -> p c r i", i=4)
+            src = raw[(j, z)].rearrange("p r (c i) -> p c r i", i=4)
             if on_vector:
                 nc.vector.tensor_copy(out=dst, in_=src)
             else:
@@ -161,14 +161,15 @@ def tile_mix_gate_over_mixed_sum_kernel(
         halves = [slice(0, T // 2), slice(T // 2, T)]
         cast(0, 0, True)
         quantise(0, 0, 1)
-        cast(0, 1, True)
-        quantise(0, 1, 2)
         cast(1, 0, True)
         quantise(1, 0, 1)
+        cast(0, 1, True)
+        quantise(0, 1, 2)
         cast(1, 1, True)
         quantise(1, 1, 2)
         g_pass(0)
         g_pass(1)
+        g_pass(2)
         q_pass(0, 0, True, False)
         q_pass(0, 1, False, False)
         a_pass(0, 0, False, False)
@@ -177,7 +178,6 @@ def tile_mix_gate_over_mixed_sum_kernel(
         a_pass(1, 1, False, False)
         q_pass(1, 0, False, False)
         q_pass(1, 1, False, True)
-        g_pass(2)
         g_pass(3)
         a_pass(2, 0, True, False)
         a_pass(2, 1, False, False)
@@ -185,11 +185,11 @@ def tile_mix_gate_over_mixed_sum_kernel(
         a_pass(3, 1, False, False)
         sigmoid(0)
         sigmoid(1)
+        sigmoid(2)
         cast(2, 0, False)
         cast(2, 1, False)
         cast(3, 0, False)
         cast(3, 1, False)
-        sigmoid(2)
         sigmoid(3)
         mul(0, everything)
         quantise(2, 0, 1)

@@ -57,8 +57,8 @@ def tile_mix_gate_over_mixed_sum_kernel(
             for j in range(j0, j1):
                 raw[(j, z)] = t[:, :, (j - j0) * P : (j - j0 + 1) * P]
 
-        xg = load_e2m1(xg_words, "xg")
         load_wq(0, 2, 0)
+        xg = load_e2m1(xg_words, "xg")
         for src, first in zip(scale_sources, first_plane):
             passes = src.shape[0]
             dst = planes[0:P:8, first * T : (first + passes) * T].bitcast(I32)
@@ -69,9 +69,10 @@ def tile_mix_gate_over_mixed_sum_kernel(
         wg = load_e4m3(wg_words, "wg")
         for r in range(1, 4):
             nc.sync.dma_start(out=planes[r:P:32, :].bitcast(I32), in_=planes[8 * r : P : 32, :].bitcast(I32))
-        load_wq(0, 2, 1)
+        load_wq(0, 1, 1)
         xq = load_e2m1(xq_words, "xq")
         wa = load_e2m1(wa_words, "wa")
+        load_wq(1, 2, 1)
         for j in range(2, TILES):
             for z in range(2):
                 load_wq(j, j + 1, z)
@@ -112,6 +113,17 @@ def tile_mix_gate_over_mixed_sum_kernel(
                 lhsT_scale=plane(1, cols),
                 rhs=xg[:, 0, :].bitcast(FP4X4),
                 rhs_scale=plane(0, everything),
+                start=True,
+                stop=True,
+            )
+
+        def warm_pass():
+            nc.tensor.matmul_mx(
+                out=p_bank[3][:, 0:P],
+                lhsT=codes[0][:, 0:P].bitcast(FP8X4),
+                lhsT_scale=made[0][:, 0:P],
+                rhs=xg[:, 0, 0 : 2 * P].bitcast(FP4X4),
+                rhs_scale=made[0][:, 0:P],
                 start=True,
                 stop=True,
             )
@@ -165,8 +177,21 @@ def tile_mix_gate_over_mixed_sum_kernel(
         quantise(1, 0, 1)
         cast(0, 1, True)
         quantise(0, 1, 2)
-        cast(1, 1, True)
-        quantise(1, 1, 2)
+        warm_pass()
+        warm_pass()
+        warm_pass()
+        warm_pass()
+        warm_pass()
+        warm_pass()
+        warm_pass()
+        warm_pass()
+        warm_pass()
+        warm_pass()
+        warm_pass()
+        warm_pass()
+        warm_pass()
+        warm_pass()
+        warm_pass()
         g_pass(0)
         g_pass(1)
         g_pass(2)
@@ -176,39 +201,41 @@ def tile_mix_gate_over_mixed_sum_kernel(
         a_pass(0, 1, False, True)
         a_pass(1, 0, True, False)
         a_pass(1, 1, False, False)
-        q_pass(1, 0, False, False)
-        q_pass(1, 1, False, True)
         g_pass(3)
-        a_pass(2, 0, True, False)
-        a_pass(2, 1, False, False)
-        a_pass(3, 0, True, False)
-        a_pass(3, 1, False, False)
+        q_pass(1, 0, False, False)
         sigmoid(0)
         sigmoid(1)
         sigmoid(2)
+        cast(1, 1, False)
         cast(2, 0, False)
         cast(2, 1, False)
         cast(3, 0, False)
         cast(3, 1, False)
         sigmoid(3)
         mul(0, everything)
-        quantise(2, 0, 1)
+        quantise(1, 1, 2)
         add(0, everything)
         store(0, everything)
-        quantise(2, 1, 2)
+        quantise(2, 0, 1)
+        q_pass(1, 1, False, True)
+        a_pass(2, 0, True, False)
+        a_pass(2, 1, False, False)
+        q_pass(2, 0, False, False)
+        a_pass(3, 0, True, False)
+        a_pass(3, 1, False, False)
         mul(1, everything)
-        quantise(3, 0, 1)
-        quantise(3, 1, 2)
+        quantise(2, 1, 2)
         add(1, everything)
         store(1, everything)
-        q_pass(2, 0, False, False)
+        quantise(3, 0, 1)
+        quantise(3, 1, 2)
         q_pass(2, 1, False, True)
         q_pass(3, 0, False, False)
         q_pass(3, 1, False, True)
         mul(2, everything)
-        mul(3, halves[0])
         add(2, everything)
         store(2, everything)
+        mul(3, halves[0])
         mul(3, halves[1])
         add(3, halves[0])
         store(3, halves[0])

@@ -18,8 +18,13 @@ ALU = mybir.AluOpType
 P = 128
 PACK = 4
 K_PASS = P * PACK
+QUADRANT = 32
+ROWS_PER_QUADRANT = 4
+LINE = 4
 TILES = N // P
+PASSES = L // K_PASS
 GATE_SHARE = 0.1
+WARM_UP_PASSES = 15
 
 
 def tile_mix_gate_over_mixed_sum_kernel(
@@ -31,78 +36,90 @@ def tile_mix_gate_over_mixed_sum_kernel(
         psum = ctx.enter_context(tc.psum_pool(name="psum", bufs=1))
         ctx.enter_context(tc.manual_schedule())
 
-        scale_sources = [xg_scales, wg_scales, xq_scales, wa_scales, xa_scales]
-        first_plane = [0, 1, 2, 4, 6]
-        planes = keep.tile([P, 8 * T], U8, name="planes", align_bytes=64)
+        scale_inputs = {"xg": xg_scales, "wg": wg_scales, "xq": xq_scales, "wa": wa_scales, "xa": xa_scales}
+        first_plane = {}
+        plane_count = 0
+        for operand, scales in scale_inputs.items():
+            first_plane[operand] = plane_count
+            plane_count = plane_count + scales.shape[0]
+        planes = keep.tile([P, plane_count * T], U8, name="planes", align_bytes=64)
         nc.vector.memset(planes[:].bitcast(I32), 0)
 
+        def plane(operand, z, cols):
+            start = (first_plane[operand] + z) * T
+            return planes[:, start + cols.start : start + cols.stop]
+
+        def load_scale_rows():
+            for operand, scales in scale_inputs.items():
+                passes = scales.shape[0]
+                first = first_plane[operand]
+                rows = planes[0:P:8, first * T : (first + passes) * T].bitcast(I32)
+                nc.sync.dma_start(
+                    out=rows.rearrange("q (z c) -> q z c", z=passes), in_=scales.bitcast(I32).rearrange("z q c -> q z c")
+                )
+
+        def place_scale_rows():
+            for r in range(1, ROWS_PER_QUADRANT):
+                nc.sync.dma_start(
+                    out=planes[r:P:QUADRANT, :].bitcast(I32), in_=planes[8 * r : P : QUADRANT, :].bitcast(I32)
+                )
+
         def load_e4m3(words, name):
-            passes = words.shape[0]
-            t = keep.tile([P, passes, T], U32, name=name, align_bytes=64)
-            nc.sync.dma_start(out=t[:].bitcast(I32), in_=words.rearrange("z p c r -> p z (c r)").bitcast(I32))
-            return t
+            tile = keep.tile([P, words.shape[0], T], U32, name=name, align_bytes=64)
+            nc.sync.dma_start(out=tile[:].bitcast(I32), in_=words.rearrange("z p c r -> p z (c r)").bitcast(I32))
+            return tile
 
         def load_e2m1(words, name):
-            passes = words.shape[0]
-            t = keep.tile([P, passes, 2 * T], U8, name=name, align_bytes=64)
-            nc.sync.dma_start(out=t[:].bitcast(I32), in_=words.rearrange("z p c -> p z c").bitcast(I32))
-            return t
+            tile = keep.tile([P, words.shape[0], 2 * T], U8, name=name, align_bytes=64)
+            nc.sync.dma_start(out=tile[:].bitcast(I32), in_=words.rearrange("z p c -> p z c").bitcast(I32))
+            return tile
 
-        raw = {}
+        wq_raw = {}
 
-        def load_wq(j0, j1, z):
-            t = keep.tile([P, PACK, (j1 - j0) * P], F32, name="raw%d%d" % (j0, z), align_bytes=64)
-            rows = wq[z * K_PASS : (z + 1) * K_PASS, j0 * P : j1 * P]
-            nc.sync.dma_start(out=t[:], in_=rows.rearrange("(p r) n -> p r n", r=PACK))
-            for j in range(j0, j1):
-                raw[(j, z)] = t[:, :, (j - j0) * P : (j - j0 + 1) * P]
+        def load_wq(tiles, z):
+            first, count = tiles[0], len(tiles)
+            tile = keep.tile([P, PACK, count * P], F32, name="wq_raw%d%d" % (first, z), align_bytes=64)
+            rows = wq[z * K_PASS : (z + 1) * K_PASS, first * P : (first + count) * P]
+            nc.sync.dma_start(out=tile[:], in_=rows.rearrange("(p r) n -> p r n", r=PACK))
+            for j in tiles:
+                wq_raw[(j, z)] = tile[:, :, (j - first) * P : (j - first + 1) * P]
 
-        load_wq(0, 2, 0)
+        load_wq((0, 1), 0)
         xg = load_e2m1(xg_words, "xg")
-        for src, first in zip(scale_sources, first_plane):
-            passes = src.shape[0]
-            dst = planes[0:P:8, first * T : (first + passes) * T].bitcast(I32)
-            nc.sync.dma_start(
-                out=dst.rearrange("q (z c) -> q z c", z=passes), in_=src.bitcast(I32).rearrange("z q c -> q z c")
-            )
+        load_scale_rows()
         xa = load_e4m3(xa_words, "xa")
         wg = load_e4m3(wg_words, "wg")
-        for r in range(1, 4):
-            nc.sync.dma_start(out=planes[r:P:32, :].bitcast(I32), in_=planes[8 * r : P : 32, :].bitcast(I32))
-        load_wq(0, 1, 1)
+        place_scale_rows()
+        load_wq((0,), 1)
         xq = load_e2m1(xq_words, "xq")
         wa = load_e2m1(wa_words, "wa")
-        load_wq(1, 2, 1)
-        for j in range(2, TILES):
-            for z in range(2):
-                load_wq(j, j + 1, z)
+        load_wq((1,), 1)
+        for j in (2, 3):
+            for z in range(PASSES):
+                load_wq((j,), z)
 
-        def plane(index, cols):
-            return planes[:, index * T + cols.start : index * T + cols.stop]
-
-        grouped = [keep.tile([P, 2, P * PACK], BF16, name="grouped%d" % j, align_bytes=64) for j in range(TILES)]
-        codes = [keep.tile([P, 2 * P], U32, name="codes%d" % j, align_bytes=64) for j in range(TILES)]
-        made = [keep.tile([P, 2 * P], U8, name="made%d" % j, align_bytes=64) for j in range(TILES)]
+        wq_bf16 = [keep.tile([P, PASSES, P * PACK], BF16, name="wq_bf16_%d" % j, align_bytes=64) for j in range(TILES)]
+        wq_codes = [keep.tile([P, PASSES * P], U32, name="wq_codes%d" % j, align_bytes=64) for j in range(TILES)]
+        wq_planes = [keep.tile([P, PASSES * P], U8, name="wq_planes%d" % j, align_bytes=64) for j in range(TILES)]
         p_bank = [psum.tile([P, T], F32, name="p%d" % j) for j in range(TILES)]
         g_bank = [psum.tile([P, T], F32, name="g%d" % j) for j in range(TILES)]
         gate = [keep.tile([P, T], F32, name="gate%d" % j) for j in range(TILES)]
         gated = [keep.tile([P, T], F32, name="gated%d" % j) for j in range(TILES)]
         result = [keep.tile([P, T], F32, name="result%d" % j) for j in range(TILES)]
-        everything = slice(0, T)
+        share = keep.tile([P, T // 2], F32, name="share")
+        all_tokens = slice(0, T)
+        halves = (slice(0, T // 2), slice(T // 2, T))
 
-        def cast(j, z, on_vector):
-            dst = grouped[j][:, z, :].rearrange("p (c i r) -> p c r i", i=4, r=PACK)
-            src = raw[(j, z)].rearrange("p r (c i) -> p c r i", i=4)
-            if on_vector:
-                nc.vector.tensor_copy(out=dst, in_=src)
-            else:
-                nc.scalar.copy(out=dst, in_=src)
+        def cast(j, z, copy):
+            dst = wq_bf16[j][:, z, :].rearrange("p (c i r) -> p c r i", i=LINE, r=PACK)
+            src = wq_raw[(j, z)].rearrange("p r (c i) -> p c r i", i=LINE)
+            copy(out=dst, in_=src)
 
-        def quantise(j, z0, z1):
+        def quantise(j, z):
             nc.vector.quantize_mx(
-                out=codes[j][:, z0 * P : z1 * P].bitcast(FP8X4),
-                scales=made[j][:, z0 * P : z1 * P],
-                in_=grouped[j][:, z0:z1, :].rearrange("p z c -> p (z c)"),
+                out=wq_codes[j][:, z * P : (z + 1) * P].bitcast(FP8X4),
+                scales=wq_planes[j][:, z * P : (z + 1) * P],
+                in_=wq_bf16[j][:, z : z + 1, :].rearrange("p z c -> p (z c)"),
             )
 
         def g_pass(j):
@@ -110,134 +127,113 @@ def tile_mix_gate_over_mixed_sum_kernel(
             nc.tensor.matmul_mx(
                 out=g_bank[j][:],
                 lhsT=wg[:, 0, cols].bitcast(FP8X4),
-                lhsT_scale=plane(1, cols),
+                lhsT_scale=plane("wg", 0, cols),
                 rhs=xg[:, 0, :].bitcast(FP4X4),
-                rhs_scale=plane(0, everything),
+                rhs_scale=plane("xg", 0, all_tokens),
                 start=True,
                 stop=True,
             )
 
-        def warm_pass():
+        def a_passes(j, opens):
+            cols = slice(j * P, (j + 1) * P)
+            for z in range(PASSES):
+                nc.tensor.matmul_mx(
+                    out=p_bank[j][:],
+                    lhsT=wa[:, z, 2 * cols.start : 2 * cols.stop].bitcast(FP4X4),
+                    lhsT_scale=plane("wa", z, cols),
+                    rhs=xa[:, z, :].bitcast(FP8X4),
+                    rhs_scale=plane("xa", z, all_tokens),
+                    start=(opens and z == 0),
+                    stop=(not opens and z == PASSES - 1),
+                )
+
+        def q_pass(j, z, start=False, stop=False):
             nc.tensor.matmul_mx(
-                out=p_bank[3][:, 0:P],
-                lhsT=codes[0][:, 0:P].bitcast(FP8X4),
-                lhsT_scale=made[0][:, 0:P],
-                rhs=xg[:, 0, 0 : 2 * P].bitcast(FP4X4),
-                rhs_scale=made[0][:, 0:P],
-                start=True,
-                stop=True,
+                out=p_bank[j][:],
+                lhsT=wq_codes[j][:, z * P : (z + 1) * P].bitcast(FP8X4),
+                lhsT_scale=wq_planes[j][:, z * P : (z + 1) * P],
+                rhs=xq[:, z, :].bitcast(FP4X4),
+                rhs_scale=plane("xq", z, all_tokens),
+                start=start,
+                stop=stop,
             )
+
+        def warm_up():
+            for count in range(WARM_UP_PASSES):
+                nc.tensor.matmul_mx(
+                    out=p_bank[TILES - 1][:, 0:P],
+                    lhsT=wq_codes[0][:, 0:P].bitcast(FP8X4),
+                    lhsT_scale=wq_planes[0][:, 0:P],
+                    rhs=xg[:, 0, 0 : 2 * P].bitcast(FP4X4),
+                    rhs_scale=wq_planes[0][:, 0:P],
+                    start=True,
+                    stop=True,
+                )
 
         def sigmoid(j):
             nc.scalar.activation(out=gate[j][:], in_=g_bank[j][:], func=ACT.Sigmoid)
 
-        def a_pass(j, z, start, stop):
-            cols = slice(j * P, (j + 1) * P)
-            nc.tensor.matmul_mx(
-                out=p_bank[j][:],
-                lhsT=wa[:, z, 2 * cols.start : 2 * cols.stop].bitcast(FP4X4),
-                lhsT_scale=plane(4 + z, cols),
-                rhs=xa[:, z, :].bitcast(FP8X4),
-                rhs_scale=plane(6 + z, everything),
-                start=start,
-                stop=stop,
+        def apply_gate(j, tokens):
+            nc.vector.tensor_tensor(
+                out=gated[j][:, tokens], in0=p_bank[j][:, tokens], in1=gate[j][:, tokens], op=ALU.mult
             )
 
-        def q_pass(j, z, start, stop):
-            nc.tensor.matmul_mx(
-                out=p_bank[j][:],
-                lhsT=codes[j][:, z * P : (z + 1) * P].bitcast(FP8X4),
-                lhsT_scale=made[j][:, z * P : (z + 1) * P],
-                rhs=xq[:, z, :].bitcast(FP4X4),
-                rhs_scale=plane(2 + z, everything),
-                start=start,
-                stop=stop,
-            )
-
-        def mul(j, cols):
-            nc.vector.tensor_tensor(out=gated[j][:, cols], in0=p_bank[j][:, cols], in1=gate[j][:, cols], op=ALU.mult)
-
-        def add(j, cols):
+        def add_share(j, tokens):
             nc.vector.scalar_tensor_tensor(
-                out=result[j][:, cols],
-                in0=g_bank[j][:, cols],
+                out=result[j][:, tokens],
+                in0=g_bank[j][:, tokens],
                 scalar=GATE_SHARE,
-                in1=gated[j][:, cols],
+                in1=gated[j][:, tokens],
                 op0=ALU.mult,
                 op1=ALU.add,
             )
 
-        def store(j, cols):
-            nc.sync.dma_start(out=out[j * P : (j + 1) * P, cols], in_=result[j][:, cols])
+        def store(j, tokens):
+            nc.sync.dma_start(out=out[j * P : (j + 1) * P, tokens], in_=result[j][:, tokens])
 
-        halves = [slice(0, T // 2), slice(T // 2, T)]
-        cast(0, 0, True)
-        quantise(0, 0, 1)
-        cast(1, 0, True)
-        quantise(1, 0, 1)
-        cast(0, 1, True)
-        quantise(0, 1, 2)
-        warm_pass()
-        warm_pass()
-        warm_pass()
-        warm_pass()
-        warm_pass()
-        warm_pass()
-        warm_pass()
-        warm_pass()
-        warm_pass()
-        warm_pass()
-        warm_pass()
-        warm_pass()
-        warm_pass()
-        warm_pass()
-        warm_pass()
-        g_pass(0)
-        g_pass(1)
-        g_pass(2)
-        q_pass(0, 0, True, False)
-        q_pass(0, 1, False, False)
-        a_pass(0, 0, False, False)
-        a_pass(0, 1, False, True)
-        a_pass(1, 0, True, False)
-        a_pass(1, 1, False, False)
+        for j, z in ((0, 0), (1, 0), (0, 1)):
+            cast(j, z, nc.vector.tensor_copy)
+            quantise(j, z)
+
+        warm_up()
+        for j in range(3):
+            g_pass(j)
+            sigmoid(j)
+        q_pass(0, 0, start=True)
+        q_pass(0, 1)
+        a_passes(0, opens=False)
+        a_passes(1, opens=True)
         g_pass(3)
-        q_pass(1, 0, False, False)
-        sigmoid(0)
-        sigmoid(1)
-        sigmoid(2)
-        cast(1, 1, False)
-        cast(2, 0, False)
-        cast(2, 1, False)
-        cast(3, 0, False)
-        cast(3, 1, False)
+        q_pass(1, 0)
+
+        for j, z in ((1, 1), (2, 0), (2, 1), (3, 0), (3, 1)):
+            cast(j, z, nc.scalar.copy)
+        nc.scalar.activation(out=share[:], in_=g_bank[2][:, halves[0]], func=ACT.Copy, scale=GATE_SHARE)
         sigmoid(3)
-        mul(0, everything)
-        quantise(1, 1, 2)
-        add(0, everything)
-        store(0, everything)
-        quantise(2, 0, 1)
-        q_pass(1, 1, False, True)
-        a_pass(2, 0, True, False)
-        a_pass(2, 1, False, False)
-        q_pass(2, 0, False, False)
-        a_pass(3, 0, True, False)
-        a_pass(3, 1, False, False)
-        mul(1, everything)
-        quantise(2, 1, 2)
-        add(1, everything)
-        store(1, everything)
-        quantise(3, 0, 1)
-        quantise(3, 1, 2)
-        q_pass(2, 1, False, True)
-        q_pass(3, 0, False, False)
-        q_pass(3, 1, False, True)
-        mul(2, everything)
-        add(2, everything)
-        store(2, everything)
-        mul(3, halves[0])
-        mul(3, halves[1])
-        add(3, halves[0])
-        store(3, halves[0])
-        add(3, halves[1])
-        store(3, halves[1])
+
+        for j in (0, 1):
+            apply_gate(j, all_tokens)
+            quantise(j + 1, 1)
+            q_pass(j + 1, 1, stop=True)
+            add_share(j, all_tokens)
+            store(j, all_tokens)
+            quantise(j + 2, 0)
+            if j == 0:
+                a_passes(2, opens=True)
+                q_pass(2, 0)
+                a_passes(3, opens=True)
+        quantise(3, 1)
+        q_pass(3, 0)
+        q_pass(3, 1, stop=True)
+
+        for tokens in halves:
+            apply_gate(2, tokens)
+        nc.gpsimd.tensor_tensor(out=result[2][:, halves[0]], in0=gated[2][:, halves[0]], in1=share[:], op=ALU.add)
+        add_share(2, halves[1])
+        store(2, all_tokens)
+
+        for tokens in halves:
+            apply_gate(3, tokens)
+        for tokens in halves:
+            add_share(3, tokens)
+            store(3, tokens)

from contextlib import ExitStack

import concourse.mybir as mybir

K, L, M, T, N = 1024, 1024, 512, 512, 512
FLOPS = 2 * (K + L + M) * T * N

F32 = mybir.dt.float32
BF16 = mybir.dt.bfloat16
I32 = mybir.dt.int32
U32 = mybir.dt.uint32
U8 = mybir.dt.uint8
FP8X4 = mybir.dt.float8_e4m3fn_x4
FP4X4 = mybir.dt.float4_e2m1fn_x4
ACT = mybir.ActivationFunctionType
ALU = mybir.AluOpType

P = 128
PACK = 4
K_PASS = P * PACK
QUADRANT = 32
ROWS_PER_QUADRANT = 4
LINE = 4
TILES = N // P
PASSES = L // K_PASS
GATE_SHARE = 0.1
WARM_UP_PASSES = 15


def tile_mix_gate_over_mixed_sum_kernel(
    tc, xa_words, xa_scales, wa_words, wa_scales, xq_words, xq_scales, wq, xg_words, xg_scales, wg_words, wg_scales, out
):
    nc = tc.nc
    with ExitStack() as ctx:
        keep = ctx.enter_context(tc.tile_pool(name="keep", bufs=1))
        psum = ctx.enter_context(tc.psum_pool(name="psum", bufs=1))
        ctx.enter_context(tc.manual_schedule())

        scale_inputs = {"xg": xg_scales, "wg": wg_scales, "xq": xq_scales, "wa": wa_scales, "xa": xa_scales}
        first_plane = {}
        plane_count = 0
        for operand, scales in scale_inputs.items():
            first_plane[operand] = plane_count
            plane_count = plane_count + scales.shape[0]
        planes = keep.tile([P, plane_count * T], U8, name="planes", align_bytes=64)
        nc.vector.memset(planes[:].bitcast(I32), 0)

        def plane(operand, z, cols):
            start = (first_plane[operand] + z) * T
            return planes[:, start + cols.start : start + cols.stop]

        def load_scale_rows():
            for operand, scales in scale_inputs.items():
                passes = scales.shape[0]
                first = first_plane[operand]
                rows = planes[0:P:8, first * T : (first + passes) * T].bitcast(I32)
                nc.sync.dma_start(
                    out=rows.rearrange("q (z c) -> q z c", z=passes), in_=scales.bitcast(I32).rearrange("z q c -> q z c")
                )

        def place_scale_rows():
            for r in range(1, ROWS_PER_QUADRANT):
                nc.sync.dma_start(
                    out=planes[r:P:QUADRANT, :].bitcast(I32), in_=planes[8 * r : P : QUADRANT, :].bitcast(I32)
                )

        def load_e4m3(words, name):
            tile = keep.tile([P, words.shape[0], T], U32, name=name, align_bytes=64)
            nc.sync.dma_start(out=tile[:].bitcast(I32), in_=words.rearrange("z p c r -> p z (c r)").bitcast(I32))
            return tile

        def load_e2m1(words, name):
            tile = keep.tile([P, words.shape[0], 2 * T], U8, name=name, align_bytes=64)
            nc.sync.dma_start(out=tile[:].bitcast(I32), in_=words.rearrange("z p c -> p z c").bitcast(I32))
            return tile

        wq_raw = {}

        def load_wq(tiles, z):
            first, count = tiles[0], len(tiles)
            tile = keep.tile([P, PACK, count * P], F32, name="wq_raw%d%d" % (first, z), align_bytes=64)
            rows = wq[z * K_PASS : (z + 1) * K_PASS, first * P : (first + count) * P]
            nc.sync.dma_start(out=tile[:], in_=rows.rearrange("(p r) n -> p r n", r=PACK))
            for j in tiles:
                wq_raw[(j, z)] = tile[:, :, (j - first) * P : (j - first + 1) * P]

        load_wq((0, 1), 0)
        xg = load_e2m1(xg_words, "xg")
        load_scale_rows()
        xa = load_e4m3(xa_words, "xa")
        wg = load_e4m3(wg_words, "wg")
        place_scale_rows()
        load_wq((0,), 1)
        xq = load_e2m1(xq_words, "xq")
        wa = load_e2m1(wa_words, "wa")
        load_wq((1,), 1)
        for j in (2, 3):
            for z in range(PASSES):
                load_wq((j,), z)

        wq_bf16 = [keep.tile([P, PASSES, P * PACK], BF16, name="wq_bf16_%d" % j, align_bytes=64) for j in range(TILES)]
        wq_codes = [keep.tile([P, PASSES * P], U32, name="wq_codes%d" % j, align_bytes=64) for j in range(TILES)]
        wq_planes = [keep.tile([P, PASSES * P], U8, name="wq_planes%d" % j, align_bytes=64) for j in range(TILES)]
        p_bank = [psum.tile([P, T], F32, name="p%d" % j) for j in range(TILES)]
        g_bank = [psum.tile([P, T], F32, name="g%d" % j) for j in range(TILES)]
        gate = [keep.tile([P, T], F32, name="gate%d" % j) for j in range(TILES)]
        gated = [keep.tile([P, T], F32, name="gated%d" % j) for j in range(TILES)]
        result = [keep.tile([P, T], F32, name="result%d" % j) for j in range(TILES)]
        share = keep.tile([P, T // 2], F32, name="share")
        all_tokens = slice(0, T)
        halves = (slice(0, T // 2), slice(T // 2, T))

        def cast(j, z, copy):
            dst = wq_bf16[j][:, z, :].rearrange("p (c i r) -> p c r i", i=LINE, r=PACK)
            src = wq_raw[(j, z)].rearrange("p r (c i) -> p c r i", i=LINE)
            copy(out=dst, in_=src)

        def quantise(j, z):
            nc.vector.quantize_mx(
                out=wq_codes[j][:, z * P : (z + 1) * P].bitcast(FP8X4),
                scales=wq_planes[j][:, z * P : (z + 1) * P],
                in_=wq_bf16[j][:, z : z + 1, :].rearrange("p z c -> p (z c)"),
            )

        def g_pass(j):
            cols = slice(j * P, (j + 1) * P)
            nc.tensor.matmul_mx(
                out=g_bank[j][:],
                lhsT=wg[:, 0, cols].bitcast(FP8X4),
                lhsT_scale=plane("wg", 0, cols),
                rhs=xg[:, 0, :].bitcast(FP4X4),
                rhs_scale=plane("xg", 0, all_tokens),
                start=True,
                stop=True,
            )

        def a_passes(j, opens):
            cols = slice(j * P, (j + 1) * P)
            for z in range(PASSES):
                nc.tensor.matmul_mx(
                    out=p_bank[j][:],
                    lhsT=wa[:, z, 2 * cols.start : 2 * cols.stop].bitcast(FP4X4),
                    lhsT_scale=plane("wa", z, cols),
                    rhs=xa[:, z, :].bitcast(FP8X4),
                    rhs_scale=plane("xa", z, all_tokens),
                    start=(opens and z == 0),
                    stop=(not opens and z == PASSES - 1),
                )

        def q_pass(j, z, start=False, stop=False):
            nc.tensor.matmul_mx(
                out=p_bank[j][:],
                lhsT=wq_codes[j][:, z * P : (z + 1) * P].bitcast(FP8X4),
                lhsT_scale=wq_planes[j][:, z * P : (z + 1) * P],
                rhs=xq[:, z, :].bitcast(FP4X4),
                rhs_scale=plane("xq", z, all_tokens),
                start=start,
                stop=stop,
            )

        def warm_up():
            for count in range(WARM_UP_PASSES):
                nc.tensor.matmul_mx(
                    out=p_bank[TILES - 1][:, 0:P],
                    lhsT=wq_codes[0][:, 0:P].bitcast(FP8X4),
                    lhsT_scale=wq_planes[0][:, 0:P],
                    rhs=xg[:, 0, 0 : 2 * P].bitcast(FP4X4),
                    rhs_scale=wq_planes[0][:, 0:P],
                    start=True,
                    stop=True,
                )

        def sigmoid(j):
            nc.scalar.activation(out=gate[j][:], in_=g_bank[j][:], func=ACT.Sigmoid)

        def apply_gate(j, tokens):
            nc.vector.tensor_tensor(
                out=gated[j][:, tokens], in0=p_bank[j][:, tokens], in1=gate[j][:, tokens], op=ALU.mult
            )

        def add_share(j, tokens):
            nc.vector.scalar_tensor_tensor(
                out=result[j][:, tokens],
                in0=g_bank[j][:, tokens],
                scalar=GATE_SHARE,
                in1=gated[j][:, tokens],
                op0=ALU.mult,
                op1=ALU.add,
            )

        def store(j, tokens):
            nc.sync.dma_start(out=out[j * P : (j + 1) * P, tokens], in_=result[j][:, tokens])

        for j, z in ((0, 0), (1, 0), (0, 1)):
            cast(j, z, nc.vector.tensor_copy)
            quantise(j, z)

        warm_up()
        for j in range(3):
            g_pass(j)
            sigmoid(j)
        q_pass(0, 0, start=True)
        q_pass(0, 1)
        a_passes(0, opens=False)
        a_passes(1, opens=True)
        g_pass(3)
        q_pass(1, 0)

        for j, z in ((1, 1), (2, 0), (2, 1), (3, 0), (3, 1)):
            cast(j, z, nc.scalar.copy)
        nc.scalar.activation(out=share[:], in_=g_bank[2][:, halves[0]], func=ACT.Copy, scale=GATE_SHARE)
        sigmoid(3)

        for j in (0, 1):
            apply_gate(j, all_tokens)
            quantise(j + 1, 1)
            q_pass(j + 1, 1, stop=True)
            add_share(j, all_tokens)
            store(j, all_tokens)
            quantise(j + 2, 0)
            if j == 0:
                a_passes(2, opens=True)
                q_pass(2, 0)
                a_passes(3, opens=True)
        quantise(3, 1)
        q_pass(3, 0)
        q_pass(3, 1, stop=True)

        for tokens in halves:
            apply_gate(2, tokens)
        nc.gpsimd.tensor_tensor(out=result[2][:, halves[0]], in0=gated[2][:, halves[0]], in1=share[:], op=ALU.add)
        add_share(2, halves[1])
        store(2, all_tokens)

        for tokens in halves:
            apply_gate(3, tokens)
        for tokens in halves:
            add_share(3, tokens)
            store(3, tokens)
